import numpy as np
import ml_dtypes


def mxq(x, axis, fmt="e4m3"):
    dtype, down = {"e4m3": (ml_dtypes.float8_e4m3fn, 7), "e5m2": (ml_dtypes.float8_e5m2, 14)}[fmt]
    v = np.moveaxis(np.asarray(x, np.float32).astype(ml_dtypes.bfloat16).astype(np.float64), axis, -1)
    blocks = v.reshape(v.shape[:-1] + (-1, 32))
    amax = np.abs(blocks).max(-1, keepdims=True)
    byte = np.maximum(np.where(amax > 0, np.frexp(amax)[1] - 1 + 127, 0) - down, 1)
    scale = np.exp2(byte - 127.0)
    codes = (blocks / scale).astype(np.float32).astype(dtype).astype(np.float64)
    return np.moveaxis((codes * scale).reshape(v.shape), -1, axis)


WIDE = False


def mx_kscale(k):
    if not WIDE:
        return np.ones(k)
    levels = np.array([30, -30])
    if k % 512:
        return np.exp2(np.random.permutation(np.resize(levels, k // 32))).repeat(32)
    a = np.empty((k // 512, 16))
    for p in range(k // 512):
        a[p, :8] = np.random.permutation(np.resize(levels, 8))
        for g in range(8):
            far = levels[np.abs(levels - a[p, g]) >= 10]
            a[p, g + 8] = far[np.random.randint(len(far))]
    return np.exp2(a.ravel()).repeat(32)


BF16 = ml_dtypes.bfloat16


def bf(x):
    return np.asarray(x, np.float32).astype(BF16)


def f64(x):
    return np.asarray(x).astype(np.float64)


E2M1 = np.array([0.0, 0.5, 1.0, 1.5, 2.0, 3.0, 4.0, 6.0, -0.0, -0.5, -1.0, -1.5, -2.0, -3.0, -4.0, -6.0])


def pack_weight(w, fmt):
    k, n = w.shape
    w = f64(bf(w)).reshape(k // 32, 32, n)
    amax = np.abs(w).max(1)
    if fmt in ("e4m3", "e5m2"):
        byte = np.frexp(amax)[1] - 1 + 127 - (7 if fmt == "e4m3" else 14)
    else:
        mant, ex = np.frexp(amax / 6.0)
        byte = np.where(mant > 0.5, ex, ex - 1) + 127
    byte = np.clip(np.where(amax > 0, byte, 1), 1, 254)
    scaled = (w * np.exp2(127.0 - byte)[:, None, :]).reshape(k, n).astype(np.float32)
    by_word = np.ascontiguousarray(scaled.reshape(k // 512, 128, 4, n).transpose(0, 1, 3, 2))
    if fmt in ("e4m3", "e5m2"):
        words = by_word.astype(ml_dtypes.float8_e4m3fn if fmt == "e4m3" else ml_dtypes.float8_e5m2).view(np.uint8)
    else:
        c = by_word.astype(ml_dtypes.float4_e2m1fn).view(np.uint8) & 0xF
        words = c[..., 0::2] | (c[..., 1::2] << 4)
    return np.ascontiguousarray(words), np.ascontiguousarray(byte.astype(np.uint8).reshape(k // 512, 16, n))


def unpack_weight(words, scales, fmt):
    g, p, n, _ = words.shape
    if fmt in ("e4m3", "e5m2"):
        vals = np.ascontiguousarray(words).view(ml_dtypes.float8_e4m3fn if fmt == "e4m3" else ml_dtypes.float8_e5m2).astype(np.float64)
    else:
        nib = np.empty((g, p, n, 4), np.uint8)
        nib[..., 0::2] = words & 0xF
        nib[..., 1::2] = words >> 4
        vals = E2M1[nib]
    vals = vals * np.repeat(np.exp2(scales.astype(np.float64) - 127.0), 8, axis=1)[..., None]
    return vals.transpose(0, 1, 3, 2).reshape(g * 512, n)

def planes(Y):
    n, m = Y.shape
    b = f64(bf(Y)).reshape(n // 32, 32, m)
    amax = np.abs(b).max(1)
    byte = np.clip(np.where(amax > 0, np.frexp(amax)[1] - 1 + 127 - 7, 1), 1, 254)
    codes = (b * np.exp2(127.0 - byte)[:, None, :]).reshape(n, m).astype(np.float32).astype(ml_dtypes.float8_e4m3fn).view(np.uint8)
    words = codes.reshape(n // 512, 128, 4, m).transpose(0, 1, 3, 2)
    return np.ascontiguousarray(words), np.ascontiguousarray(byte.astype(np.uint8).reshape(n // 512, 16, m))


A, D, C, T, K = 2048, 1024, 3, 512, 1536
TAIL = 0.8
EXTENT = np.array([0.8, 0.8, 0.3])
OFFSET = np.array([0.0, 0.0, 1.0])


def setup_inputs():
    s = mx_kscale(K)
    bright = np.exp(TAIL * np.random.randn(1, T, D) - TAIL ** 2)
    G = (np.random.randn(C, T, D) * bright).reshape(K, D)
    g_words, g_scales = pack_weight(G * s[:, None], "e5m2")
    acc = np.random.randn(A, K) / np.sqrt(K)
    pos_d = np.random.uniform(-0.5, 0.5, (D, C)) * EXTENT
    pos_a = np.random.uniform(-0.5, 0.5, (A, C)) * EXTENT + OFFSET
    r2 = ((pos_a[:, None, :] - pos_d[None, :, :]) ** 2).sum(axis=2)
    pop = 2.0 * np.exp(0.8 * np.random.randn(D))
    return {"g_words": g_words, "g_scales": g_scales,
            "acceptor_dipoles": bf(acc / s[None, :]),
            "inv6": bf(1.0 / r2 ** 3), "donor_pop": bf(pop)}


def reference(g_words, g_scales, acceptor_dipoles, inv6, donor_pop):
    G = unpack_weight(g_words, g_scales, "e5m2")
    acc = mxq(f64(acceptor_dipoles), 1, "e4m3")
    V = acc @ G
    y = V * V * f64(inv6) * f64(donor_pop)
    Y = y.T
    words, scales = planes(Y)
    return y, words, scales

@@ -1,0 +1,227 @@
+from contextlib import ExitStack
+
+import concourse.mybir as mybir
+from concourse.masks import make_identity
+
+A, D, K = 2048, 1024, 1536
+FLOPS = 2 * A * D * K
+
+F32 = mybir.dt.float32
+BF16 = mybir.dt.bfloat16
+I32 = mybir.dt.int32
+U32 = mybir.dt.uint32
+U8 = mybir.dt.uint8
+E4M3X4 = mybir.dt.float8_e4m3fn_x4
+E5M2X4 = mybir.dt.float8_e5m2_x4
+SQUARE = mybir.ActivationFunctionType.Square
+MULT = mybir.AluOpType.mult
+
+P = 128
+TILES = A // P
+KG = K // 512
+DG = D // 512
+STORE_TILES = 4
+
+
+def tile_dipole_gram_transfer_flow_k2_kernel(
+    tc, g_words, g_scales, acceptor_dipoles, inv6, donor_pop, out_0, out_1, out_2
+):
+    nc = tc.nc
+    with ExitStack() as ctx:
+        sb = ctx.enter_context(tc.tile_pool(name="sb", bufs=1))
+        ps = ctx.enter_context(tc.psum_pool(name="ps", bufs=1))
+
+        def ring(pool, label, count, shape, dtype):
+            tiles = []
+            for j in range(count):
+                t = pool.tile(shape, dtype, name="%s%d" % (label, j), align_bytes=64)
+                tiles.append(t)
+            return tiles
+
+        def bank_ring(label, count, shape):
+            tiles = []
+            for j in range(count):
+                t = ps.tile(shape, F32, name="%s%d" % (label, j))
+                tiles.append(t)
+            return tiles
+
+        ident = sb.tile([P, P], F32, name="ident", align_bytes=64)
+        pop_rows = sb.tile([P, 8], BF16, name="pop_rows", align_bytes=64)
+        pop_all = sb.tile([P, D], BF16, name="pop_all", align_bytes=64)
+        g_codes = ring(sb, "g_codes", DG, [P, KG, 512], U32)
+        g_sc = sb.tile([P, KG, D], U8, name="g_sc", align_bytes=64)
+        acc_raw = ring(sb, "acc_raw", TILES, [P, K], BF16)
+        inv_raw = ring(sb, "inv_raw", TILES, [P, D], BF16)
+        acc_grp = ring(sb, "acc_grp", 3, [P, KG, P, 4], BF16)
+        acc_codes = ring(sb, "acc_codes", 3, [P, KG, P], U32)
+        acc_sc = ring(sb, "acc_sc", 3, [P, KG, P], U8)
+        weight = ring(sb, "weight", 4, [P, D], F32)
+        square = ring(sb, "square", 2, [P, D], F32)
+        y32 = ring(sb, "y32_", 8, [P, D], F32)
+        y16 = ring(sb, "y16_", 3, [P, DG, 512], BF16)
+        y_grp = ring(sb, "y_grp", 3, [P, DG, P, 4], BF16)
+        y_codes = sb.tile([P, DG, A], U32, name="y_codes", align_bytes=64)
+        y_sc = sb.tile([P, DG, A], U8, name="y_sc", align_bytes=64)
+
+        acc_bank01 = ps.tile([P, 2, 2, P], F32, name="acc_bank01")
+        acc_bank2 = ps.tile([P, 2, P], F32, name="acc_bank2")
+        y_bank = bank_ring("y_bank", 2, [P, DG, 2, P])
+        v_bank = bank_ring("v_bank", 4, [P, 512])
+
+        make_identity(nc, ident[:])
+
+        def rows(i):
+            return slice(i * P, (i + 1) * P)
+
+        def load_acc(i):
+            nc.sync.dma_start(out=acc_raw[i][:], in_=acceptor_dipoles[rows(i), :])
+
+        def load_inv(i):
+            nc.sync.dma_start(out=inv_raw[i][:], in_=inv6[rows(i), :])
+
+        def load_g(h):
+            src = g_words.rearrange("g p n t -> p g (n t)")[:, :, 2048 * h : 2048 * (h + 1)]
+            nc.sync.dma_start(out=g_codes[h][:].bitcast(I32), in_=src.bitcast(I32))
+
+        def transpose_acc(i):
+            words = acc_raw[i][:].bitcast(F32)
+            for g in range(KG):
+                for u in range(2):
+                    dst = acc_bank01[:, g, u, :] if g < 2 else acc_bank2[:, u, :]
+                    nc.tensor.transpose(dst, words[:, 256 * g + u : 256 * (g + 1) : 2], ident[:])
+
+        def copy_acc(i):
+            grp = acc_grp[i % 3][:].bitcast(F32)
+            nc.scalar.copy(out=grp[:, 0:2, :, :], in_=acc_bank01[:].rearrange("p g u m -> p g m u"))
+            nc.scalar.copy(out=grp[:, 2, :, :], in_=acc_bank2[:].rearrange("p u m -> p m u"))
+
+        def quantize_acc(i):
+            src = acc_grp[i % 3][:].rearrange("p g m t -> p (g m t)")
+            codes = acc_codes[i % 3][:].rearrange("p g m -> p (g m)")
+            scales = acc_sc[i % 3][:].rearrange("p g m -> p (g m)")
+            for lo, hi in ((0, 2 * P), (2 * P, 3 * P)):
+                nc.vector.quantize_mx(
+                    out=codes[:, lo:hi].bitcast(E4M3X4), scales=scales[:, lo:hi], in_=src[:, 4 * lo : 4 * hi]
+                )
+
+        def multiply(i, h):
+            for g in range(KG):
+                nc.tensor.matmul_mx(
+                    out=v_bank[(2 * i + h) % 4][:],
+                    lhsT=acc_codes[i % 3][:, g, :].bitcast(E4M3X4),
+                    lhsT_scale=acc_sc[i % 3][:, g, :],
+                    rhs=g_codes[h][:, g, :].bitcast(E5M2X4),
+                    rhs_scale=g_sc[:, g, 512 * h : 512 * (h + 1)],
+                    start=(g == 0),
+                    stop=(g == KG - 1),
+                )
+
+        def make_weight(i):
+            nc.vector.tensor_tensor(out=weight[i % 4][:], in0=inv_raw[i][:], in1=pop_all[:], op=MULT)
+
+        def square_v(i, h):
+            nc.scalar.activation(
+                out=square[i % 2][:, 512 * h : 512 * (h + 1)], in_=v_bank[(2 * i + h) % 4][:], func=SQUARE
+            )
+
+        def make_y(i):
+            nc.vector.tensor_tensor(out=y32[i % 8][:], in0=square[i % 2][:], in1=weight[i % 4][:], op=MULT)
+
+        def store_y(i):
+            nc.sync.dma_start(out=out_0[rows(i), :], in_=y32[i % 8][:])
+
+        def round_y(i, g):
+            src = y32[i % 8][:, 512 * g : 512 * (g + 1)].rearrange("a (p u e) -> a u p e", u=2, e=2)
+            dst = y16[i % 3][:, g, :].rearrange("a (u p e) -> a u p e", u=2, e=2)
+            if g == 0:
+                nc.vector.tensor_copy(out=dst, in_=src)
+            else:
+                nc.scalar.copy(out=dst, in_=src)
+
+        def transpose_y(i):
+            words = y16[i % 3][:].bitcast(F32)
+            for g in range(DG):
+                for u in range(2):
+                    nc.tensor.transpose(y_bank[i % 2][:, g, u, :], words[:, g, P * u : P * (u + 1)], ident[:])
+
+        def copy_y(i):
+            nc.scalar.copy(out=y_grp[i % 3][:].bitcast(F32), in_=y_bank[i % 2][:].rearrange("p g u m -> p g m u"))
+
+        def quantize_y(i):
+            for g in range(DG):
+                nc.vector.quantize_mx(
+                    out=y_codes[:, g, rows(i)].bitcast(E4M3X4),
+                    scales=y_sc[:, g, rows(i)],
+                    in_=y_grp[i % 3][:, g, :, :].rearrange("p m t -> p (m t)"),
+                )
+
+        def store_codes(lo, hi):
+            dst = out_1.rearrange("g p m t -> p g (m t)")[:, :, 4 * P * lo : 4 * P * hi]
+            nc.sync.dma_start(out=dst.bitcast(I32), in_=y_codes[:, :, P * lo : P * hi].bitcast(I32))
+
+        with tc.manual_schedule():
+            nc.vector.memset(g_sc[:].bitcast(I32), 0)
+            nc.sync.dma_start(out=pop_rows[:], in_=donor_pop.rearrange("(p j) -> p j", j=8))
+            load_acc(0)
+            for q in range(4):
+                nc.scalar.dma_start(
+                    out=g_sc[32 * q : 32 * q + 4, :, :].bitcast(I32),
+                    in_=g_scales[:, 4 * q : 4 * q + 4, :].rearrange("g r n -> r g n").bitcast(I32),
+                )
+            load_inv(0)
+            load_g(0)
+            load_acc(1)
+            load_inv(1)
+            load_g(1)
+            for i in range(2, TILES):
+                load_acc(i)
+                load_inv(i)
+
+            pop_words = pop_rows[:].bitcast(F32)
+            pop_bank = y_bank[1][:].rearrange("p g u m -> p (g u) m")
+            for j in range(4):
+                nc.tensor.transpose(pop_bank[:, j, :], pop_words[:, j : j + 1].to_broadcast([P, P]), ident[:])
+            nc.vector.tensor_copy(
+                out=pop_all[:].bitcast(F32).rearrange("p (n j) -> p n j", j=4),
+                in_=pop_bank.rearrange("p j n -> p n j"),
+            )
+
+            def live(i):
+                return 0 <= i < TILES
+
+            for s in range(-2, TILES + 4):
+                if live(s + 2):
+                    transpose_acc(s + 2)
+                if live(s - 3):
+                    transpose_y(s - 3)
+                if live(s - 1):
+                    square_v(s - 1, 0)
+                    square_v(s - 1, 1)
+                if live(s + 1):
+                    quantize_acc(s + 1)
+                if live(s + 2):
+                    make_weight(s + 2)
+                if live(s):
+                    multiply(s, 0)
+                    multiply(s, 1)
+                if live(s + 2):
+                    copy_acc(s + 2)
+                if live(s - 2):
+                    round_y(s - 2, 0)
+                    round_y(s - 2, 1)
+                if live(s - 3):
+                    copy_y(s - 3)
+                if live(s - 4):
+                    quantize_y(s - 4)
+                if live(s - 1):
+                    make_y(s - 1)
+                    store_y(s - 1)
+                if live(s - 4) and (s - 4) % STORE_TILES == STORE_TILES - 1:
+                    store_codes(s - 4 - (STORE_TILES - 1), s - 3)
+
+            for q in range(4):
+                eng = nc.scalar if q % 2 else nc.sync
+                eng.dma_start(
+                    out=out_2[:, 4 * q : 4 * q + 4, :].rearrange("g r m -> r g m").bitcast(I32),
+                    in_=y_sc[32 * q : 32 * q + 4, :, :].bitcast(I32),
+                )

@@ -20,7 +20,14 @@ P = 128
 TILES = A // P
 KG = K // 512
 DG = D // 512
-STORE_TILES = 4
+NU = 12
+NW = 8
+NS = 4
+NY = 8
+NR = 4
+NA = 12
+CODE_GROUPS = ((0, 4), (4, 8), (8, 12), (12, 14), (14, 16))
+SCALE_GROUPS = ((0, 12), (12, 16))
 
 
 def tile_dipole_gram_transfer_flow_k2_kernel(
@@ -31,136 +38,159 @@ def tile_dipole_gram_transfer_flow_k2_kernel(
         sb = ctx.enter_context(tc.tile_pool(name="sb", bufs=1))
         ps = ctx.enter_context(tc.psum_pool(name="ps", bufs=1))
 
-        def ring(pool, label, count, shape, dtype):
-            tiles = []
-            for j in range(count):
-                t = pool.tile(shape, dtype, name="%s%d" % (label, j), align_bytes=64)
-                tiles.append(t)
-            return tiles
+        def sbuf(label, shape, dtype):
+            t = sb.tile(shape, dtype, name=label, align_bytes=64)
+            return t
 
-        def bank_ring(label, count, shape):
-            tiles = []
-            for j in range(count):
-                t = ps.tile(shape, F32, name="%s%d" % (label, j))
-                tiles.append(t)
-            return tiles
+        def bank(label):
+            t = ps.tile([P, 512], F32, name=label)
+            return t
 
-        ident = sb.tile([P, P], F32, name="ident", align_bytes=64)
-        pop_rows = sb.tile([P, 8], BF16, name="pop_rows", align_bytes=64)
-        pop_all = sb.tile([P, D], BF16, name="pop_all", align_bytes=64)
-        g_codes = ring(sb, "g_codes", DG, [P, KG, 512], U32)
-        g_sc = sb.tile([P, KG, D], U8, name="g_sc", align_bytes=64)
-        acc_raw = ring(sb, "acc_raw", TILES, [P, K], BF16)
-        inv_raw = ring(sb, "inv_raw", TILES, [P, D], BF16)
-        acc_grp = ring(sb, "acc_grp", 3, [P, KG, P, 4], BF16)
-        acc_codes = ring(sb, "acc_codes", 3, [P, KG, P], U32)
-        acc_sc = ring(sb, "acc_sc", 3, [P, KG, P], U8)
-        weight = ring(sb, "weight", 4, [P, D], F32)
-        square = ring(sb, "square", 2, [P, D], F32)
-        y32 = ring(sb, "y32_", 8, [P, D], F32)
-        y16 = ring(sb, "y16_", 3, [P, DG, 512], BF16)
-        y_grp = ring(sb, "y_grp", 3, [P, DG, P, 4], BF16)
-        y_codes = sb.tile([P, DG, A], U32, name="y_codes", align_bytes=64)
-        y_sc = sb.tile([P, DG, A], U8, name="y_sc", align_bytes=64)
+        ident = sbuf("ident", [P, P], F32)
+        pop_rows = sbuf("pop_rows", [P, 8], BF16)
+        pop_all = sbuf("pop_all", [P, 1, D], BF16)
+        g_codes = [sbuf("g_codes%d" % h, [P, KG, 512], U32) for h in range(DG)]
+        g_sc = sbuf("g_sc", [P, KG, D], U8)
+        acc_raw = sbuf("acc_raw", [P, NA, K], BF16)
+        inv_raw = sbuf("inv_raw", [P, TILES, D], BF16)
+        acc_grp = sbuf("acc_grp", [P, NU, P, 4], BF16)
+        acc_codes = sbuf("acc_codes", [P, NU, P], U32)
+        acc_sc = sbuf("acc_sc", [P, NU, P], U8)
+        weight = sbuf("weight", [P, NW, D], F32)
+        square = sbuf("square", [P, NS, D], F32)
+        y32 = sbuf("y32", [P, NY, D], F32)
+        y16 = sbuf("y16", [P, NR, D], BF16)
+        y_grp = [sbuf("y_grp%d" % j, [P, DG, 2 * P, 4], BF16) for j in range(2)]
+        y_codes = {}
+        for lo, hi in CODE_GROUPS:
+            t = sbuf("y_codes%d" % lo, [P, DG, P * (hi - lo)], U32)
+            for i in range(lo, hi):
+                y_codes[i] = (t, lo)
+        y_sc = {}
+        for lo, hi in SCALE_GROUPS:
+            t = sbuf("y_sc%d" % lo, [P, DG, P * (hi - lo)], U8)
+            for i in range(lo, hi):
+                y_sc[i] = (t, lo)
 
-        acc_bank01 = ps.tile([P, 2, 2, P], F32, name="acc_bank01")
-        acc_bank2 = ps.tile([P, 2, P], F32, name="acc_bank2")
-        y_bank = bank_ring("y_bank", 2, [P, DG, 2, P])
-        v_bank = bank_ring("v_bank", 4, [P, 512])
+        acc_bank = [bank("acc_bank%d" % j) for j in range(3)]
+        y_bank = [bank("y_bank%d" % j) for j in range(2)]
+        v_bank = [bank("v_bank%d" % j) for j in range(3)]
 
-        make_identity(nc, ident[:])
-
-        def rows(i):
-            return slice(i * P, (i + 1) * P)
+        def rows(i, n=1):
+            return slice(i * P, (i + n) * P)
 
         def load_acc(i):
-            nc.sync.dma_start(out=acc_raw[i][:], in_=acceptor_dipoles[rows(i), :])
+            nc.sync.dma_start(out=acc_raw[:, i % NA, :], in_=acceptor_dipoles[rows(i), :])
 
         def load_inv(i):
-            nc.sync.dma_start(out=inv_raw[i][:], in_=inv6[rows(i), :])
+            nc.sync.dma_start(out=inv_raw[:, i, :], in_=inv6[rows(i), :])
 
         def load_g(h):
             src = g_words.rearrange("g p n t -> p g (n t)")[:, :, 2048 * h : 2048 * (h + 1)]
             nc.sync.dma_start(out=g_codes[h][:].bitcast(I32), in_=src.bitcast(I32))
 
-        def transpose_acc(i):
-            words = acc_raw[i][:].bitcast(F32)
-            for g in range(KG):
+        def transpose_acc(n0, n1):
+            for n in range(n0, n1):
+                i, g = divmod(n, KG)
+                words = acc_raw[:, i % NA, :].bitcast(F32)
                 for u in range(2):
-                    dst = acc_bank01[:, g, u, :] if g < 2 else acc_bank2[:, u, :]
-                    nc.tensor.transpose(dst, words[:, 256 * g + u : 256 * (g + 1) : 2], ident[:])
+                    col = P * (2 * (n % 2) + u)
+                    nc.tensor.transpose(
+                        acc_bank[(n // 2) % 3][:, col : col + P], words[:, 256 * g + u : 256 * (g + 1) : 2], ident[:]
+                    )
 
-        def copy_acc(i):
-            grp = acc_grp[i % 3][:].bitcast(F32)
-            nc.scalar.copy(out=grp[:, 0:2, :, :], in_=acc_bank01[:].rearrange("p g u m -> p g m u"))
-            nc.scalar.copy(out=grp[:, 2, :, :], in_=acc_bank2[:].rearrange("p u m -> p m u"))
+        def copy_acc(n0, n1):
+            src = acc_bank[(n0 // 2) % 3][:].rearrange("p (n u m) -> p n m u", n=2, u=2)
+            dst = acc_grp[:].bitcast(F32)
+            nc.scalar.copy(out=dst[:, n0 % NU : n0 % NU + n1 - n0, :, :], in_=src[:, n0 % 2 : n0 % 2 + n1 - n0, :, :])
 
-        def quantize_acc(i):
-            src = acc_grp[i % 3][:].rearrange("p g m t -> p (g m t)")
-            codes = acc_codes[i % 3][:].rearrange("p g m -> p (g m)")
-            scales = acc_sc[i % 3][:].rearrange("p g m -> p (g m)")
-            for lo, hi in ((0, 2 * P), (2 * P, 3 * P)):
-                nc.vector.quantize_mx(
-                    out=codes[:, lo:hi].bitcast(E4M3X4), scales=scales[:, lo:hi], in_=src[:, 4 * lo : 4 * hi]
-                )
+        def quantize_acc(n0, n1):
+            span = slice(n0 % NU, n0 % NU + n1 - n0)
+            nc.vector.quantize_mx(
+                out=acc_codes[:, span, :].rearrange("p n m -> p (n m)").bitcast(E4M3X4),
+                scales=acc_sc[:, span, :].rearrange("p n m -> p (n m)"),
+                in_=acc_grp[:, span, :, :].rearrange("p n m t -> p (n m t)"),
+            )
 
         def multiply(i, h):
             for g in range(KG):
+                n = (KG * i + g) % NU
                 nc.tensor.matmul_mx(
-                    out=v_bank[(2 * i + h) % 4][:],
-                    lhsT=acc_codes[i % 3][:, g, :].bitcast(E4M3X4),
-                    lhsT_scale=acc_sc[i % 3][:, g, :],
+                    out=v_bank[(2 * i + h) % 3][:],
+                    lhsT=acc_codes[:, n, :].bitcast(E4M3X4),
+                    lhsT_scale=acc_sc[:, n, :],
                     rhs=g_codes[h][:, g, :].bitcast(E5M2X4),
                     rhs_scale=g_sc[:, g, 512 * h : 512 * (h + 1)],
                     start=(g == 0),
                     stop=(g == KG - 1),
                 )
 
-        def make_weight(i):
-            nc.vector.tensor_tensor(out=weight[i % 4][:], in0=inv_raw[i][:], in1=pop_all[:], op=MULT)
+        def make_weight(i, n):
+            nc.vector.tensor_tensor(
+                out=weight[:, i % NW : i % NW + n, :],
+                in0=inv_raw[:, i : i + n, :],
+                in1=pop_all[:].to_broadcast([P, n, D]),
+                op=MULT,
+            )
 
         def square_v(i, h):
             nc.scalar.activation(
-                out=square[i % 2][:, 512 * h : 512 * (h + 1)], in_=v_bank[(2 * i + h) % 4][:], func=SQUARE
+                out=square[:, i % NS, 512 * h : 512 * (h + 1)], in_=v_bank[(2 * i + h) % 3][:], func=SQUARE
             )
 
-        def make_y(i):
-            nc.vector.tensor_tensor(out=y32[i % 8][:], in0=square[i % 2][:], in1=weight[i % 4][:], op=MULT)
+        def make_y(i, lo=0, hi=D):
+            nc.vector.tensor_tensor(
+                out=y32[:, i % NY, lo:hi], in0=square[:, i % NS, lo:hi], in1=weight[:, i % NW, lo:hi], op=MULT
+            )
 
-        def store_y(i):
-            nc.sync.dma_start(out=out_0[rows(i), :], in_=y32[i % 8][:])
+        def store_y(i, lo=0, hi=D):
+            nc.sync.dma_start(out=out_0[rows(i), lo:hi], in_=y32[:, i % NY, lo:hi])
 
-        def round_y(i, g):
-            src = y32[i % 8][:, 512 * g : 512 * (g + 1)].rearrange("a (p u e) -> a u p e", u=2, e=2)
-            dst = y16[i % 3][:, g, :].rearrange("a (u p e) -> a u p e", u=2, e=2)
-            if g == 0:
+        def round_y(i, g0, g1, on_vector):
+            src = y32[:, i % NY, 512 * g0 : 512 * g1].rearrange("a (g p u e) -> a g u p e", p=P, u=2, e=2)
+            dst = y16[:, i % NR, 512 * g0 : 512 * g1].rearrange("a (g u p e) -> a g u p e", p=P, u=2, e=2)
+            if g1 - g0 == 1:
+                src = src[:, 0, :, :, :]
+                dst = dst[:, 0, :, :, :]
+            if on_vector:
                 nc.vector.tensor_copy(out=dst, in_=src)
             else:
                 nc.scalar.copy(out=dst, in_=src)
 
-        def transpose_y(i):
-            words = y16[i % 3][:].bitcast(F32)
-            for g in range(DG):
-                for u in range(2):
-                    nc.tensor.transpose(y_bank[i % 2][:, g, u, :], words[:, g, P * u : P * (u + 1)], ident[:])
+        def transpose_y(i, g0=0, g1=DG):
+            words = y16[:, i % NR, :].bitcast(F32)
+            for c in range(2 * g0, 2 * g1):
+                nc.tensor.transpose(y_bank[i % 2][:, P * c : P * (c + 1)], words[:, P * c : P * (c + 1)], ident[:])
 
-        def copy_y(i):
-            nc.scalar.copy(out=y_grp[i % 3][:].bitcast(F32), in_=y_bank[i % 2][:].rearrange("p g u m -> p g m u"))
+        def copy_y(i, g0=0, g1=DG):
+            dst = y_grp[(i // 2) % 2][:].bitcast(F32)[:, g0:g1, rows(i % 2), :]
+            src = y_bank[i % 2][:].rearrange("p (g u m) -> p g m u", g=DG, u=2)[:, g0:g1, :, :]
+            nc.scalar.copy(out=dst, in_=src)
 
-        def quantize_y(i):
-            for g in range(DG):
+        def quantize_y(i, n, g0=0, g1=DG):
+            codes, code_lo = y_codes[i]
+            scales, scale_lo = y_sc[i]
+            for g in range(g0, g1):
                 nc.vector.quantize_mx(
-                    out=y_codes[:, g, rows(i)].bitcast(E4M3X4),
-                    scales=y_sc[:, g, rows(i)],
-                    in_=y_grp[i % 3][:, g, :, :].rearrange("p m t -> p (m t)"),
+                    out=codes[:, g, rows(i - code_lo, n)].bitcast(E4M3X4),
+                    scales=scales[:, g, rows(i - scale_lo, n)],
+                    in_=y_grp[(i // 2) % 2][:, g, rows(i % 2, n), :].rearrange("p m t -> p (m t)"),
                 )
 
         def store_codes(lo, hi):
             dst = out_1.rearrange("g p m t -> p g (m t)")[:, :, 4 * P * lo : 4 * P * hi]
-            nc.sync.dma_start(out=dst.bitcast(I32), in_=y_codes[:, :, P * lo : P * hi].bitcast(I32))
+            nc.sync.dma_start(out=dst.bitcast(I32), in_=y_codes[lo][0][:].bitcast(I32))
+
+        def store_scales(lo, hi, engines):
+            for q in range(4):
+                engines[q % len(engines)].dma_start(
+                    out=out_2[:, 4 * q : 4 * q + 4, P * lo : P * hi].rearrange("g r m -> r g m").bitcast(I32),
+                    in_=y_sc[lo][0][32 * q : 32 * q + 4, :, :].bitcast(I32),
+                )
 
         with tc.manual_schedule():
             nc.vector.memset(g_sc[:].bitcast(I32), 0)
+            make_identity(nc, ident[:])
             nc.sync.dma_start(out=pop_rows[:], in_=donor_pop.rearrange("(p j) -> p j", j=8))
             load_acc(0)
             for q in range(4):
@@ -169,59 +199,203 @@ def tile_dipole_gram_transfer_flow_k2_kernel(
                     in_=g_scales[:, 4 * q : 4 * q + 4, :].rearrange("g r n -> r g n").bitcast(I32),
                 )
             load_inv(0)
-            load_g(0)
             load_acc(1)
+            load_acc(2)
+            load_g(0)
             load_inv(1)
+            load_inv(2)
+            load_inv(3)
+            load_acc(3)
             load_g(1)
-            for i in range(2, TILES):
-                load_acc(i)
-                load_inv(i)
+            load_inv(4)
+            load_acc(4)
+            load_acc(5)
+            load_inv(5)
+            load_inv(6)
+            load_inv(7)
+            load_acc(6)
+            load_acc(7)
+            load_acc(8)
+            load_inv(8)
+            load_acc(9)
+            load_inv(9)
+            load_acc(10)
+            load_inv(10)
+            load_acc(11)
+            load_inv(11)
+            load_inv(12)
+            load_inv(13)
+            load_inv(14)
+            load_inv(15)
 
             pop_words = pop_rows[:].bitcast(F32)
-            pop_bank = y_bank[1][:].rearrange("p g u m -> p (g u) m")
             for j in range(4):
-                nc.tensor.transpose(pop_bank[:, j, :], pop_words[:, j : j + 1].to_broadcast([P, P]), ident[:])
-            nc.vector.tensor_copy(
-                out=pop_all[:].bitcast(F32).rearrange("p (n j) -> p n j", j=4),
-                in_=pop_bank.rearrange("p j n -> p n j"),
+                nc.tensor.transpose(
+                    y_bank[1][:, P * j : P * (j + 1)], pop_words[:, j : j + 1].to_broadcast([P, P]), ident[:]
+                )
+            nc.scalar.copy(
+                out=pop_all[:, 0, :].bitcast(F32).rearrange("p (n j) -> p n j", j=4),
+                in_=y_bank[1][:].rearrange("p (j n) -> p n j", j=4),
             )
 
-            def live(i):
-                return 0 <= i < TILES
-
-            for s in range(-2, TILES + 4):
-                if live(s + 2):
-                    transpose_acc(s + 2)
-                if live(s - 3):
-                    transpose_y(s - 3)
-                if live(s - 1):
-                    square_v(s - 1, 0)
-                    square_v(s - 1, 1)
-                if live(s + 1):
-                    quantize_acc(s + 1)
-                if live(s + 2):
-                    make_weight(s + 2)
-                if live(s):
-                    multiply(s, 0)
-                    multiply(s, 1)
-                if live(s + 2):
-                    copy_acc(s + 2)
-                if live(s - 2):
-                    round_y(s - 2, 0)
-                    round_y(s - 2, 1)
-                if live(s - 3):
-                    copy_y(s - 3)
-                if live(s - 4):
-                    quantize_y(s - 4)
-                if live(s - 1):
-                    make_y(s - 1)
-                    store_y(s - 1)
-                if live(s - 4) and (s - 4) % STORE_TILES == STORE_TILES - 1:
-                    store_codes(s - 4 - (STORE_TILES - 1), s - 3)
-
-            for q in range(4):
-                eng = nc.scalar if q % 2 else nc.sync
-                eng.dma_start(
-                    out=out_2[:, 4 * q : 4 * q + 4, :].rearrange("g r m -> r g m").bitcast(I32),
-                    in_=y_sc[32 * q : 32 * q + 4, :, :].bitcast(I32),
-                )
+            transpose_acc(0, 6)
+            copy_acc(0, 2)
+            copy_acc(2, 4)
+            copy_acc(4, 6)
+            make_weight(0, 1)
+            quantize_acc(0, 2)
+            quantize_acc(2, 4)
+            transpose_acc(6, 8)
+            copy_acc(6, 8)
+            quantize_acc(4, 6)
+            make_weight(1, 1)
+            multiply(0, 0)
+            multiply(1, 0)
+            transpose_acc(8, 12)
+            square_v(0, 0)
+            square_v(1, 0)
+            make_weight(2, 1)
+            make_weight(3, 1)
+            copy_acc(8, 10)
+            copy_acc(10, 12)
+            make_y(0, 0, 512)
+            make_y(1, 0, 512)
+            quantize_acc(6, 8)
+            quantize_acc(8, 12)
+            multiply(0, 1)
+            multiply(1, 1)
+            transpose_acc(12, 18)
+            round_y(0, 0, 1, False)
+            square_v(0, 1)
+            round_y(1, 0, 1, False)
+            square_v(1, 1)
+            make_weight(4, 1)
+            make_y(0, 512, D)
+            make_y(1, 512, D)
+            store_y(0)
+            store_y(1)
+            copy_acc(12, 14)
+            copy_acc(14, 16)
+            round_y(0, 1, 2, False)
+            copy_acc(16, 18)
+            multiply(2, 0)
+            square_v(2, 0)
+            multiply(2, 1)
+            round_y(1, 1, 2, False)
+            square_v(2, 1)
+            multiply(3, 0)
+            multiply(3, 1)
+            square_v(3, 0)
+            square_v(3, 1)
+            make_weight(5, 1)
+            quantize_acc(12, 14)
+            make_weight(6, 2)
+            quantize_acc(14, 18)
+            make_y(2)
+            make_y(3)
+            store_y(2)
+            store_y(3)
+            for j in range(2, 6):
+                a, b, n = 2 * j, 2 * j + 1, 6 * j
+                transpose_acc(n + 6, n + 12)
+                transpose_y(a - 4)
+                transpose_y(b - 4)
+                copy_acc(n + 6, n + 8)
+                copy_acc(n + 8, n + 10)
+                copy_acc(n + 10, n + 12)
+                round_y(a - 2, 0, 1, False)
+                round_y(a - 2, 1, 2, False)
+                quantize_acc(n + 6, n + 8)
+                round_y(b - 2, 0, 2, True)
+                make_weight(a + 4, 2)
+                quantize_acc(n + 8, n + 12)
+                multiply(a, 0)
+                square_v(a, 0)
+                multiply(a, 1)
+                copy_y(b - 4)
+                square_v(a, 1)
+                copy_y(a - 4)
+                multiply(b, 0)
+                multiply(b, 1)
+                square_v(b, 0)
+                square_v(b, 1)
+                make_y(a)
+                store_y(a)
+                quantize_y(a - 4, 2)
+                if j % 2 == 1:
+                    store_codes(a - 6, a - 2)
+                make_y(b)
+                store_y(b)
+                if j < 4:
+                    load_acc(a + 8)
+                    load_acc(b + 8)
+            transpose_acc(42, 48)
+            transpose_y(8)
+            transpose_y(9)
+            copy_acc(42, 44)
+            copy_acc(44, 46)
+            copy_acc(46, 48)
+            round_y(10, 0, 1, True)
+            quantize_acc(42, 44)
+            round_y(11, 0, 2, True)
+            quantize_acc(44, 48)
+            round_y(10, 1, 2, False)
+            multiply(12, 0)
+            square_v(12, 0)
+            multiply(12, 1)
+            copy_y(8)
+            square_v(12, 1)
+            multiply(13, 0)
+            multiply(13, 1)
+            square_v(13, 0)
+            square_v(13, 1)
+            copy_y(9)
+            transpose_y(10)
+            make_y(12)
+            store_y(12)
+            make_y(13)
+            store_y(13)
+            quantize_y(8, 2)
+            multiply(14, 0)
+            multiply(14, 1)
+            copy_y(10)
+            square_v(14, 0)
+            square_v(14, 1)
+            transpose_y(11)
+            multiply(15, 0)
+            round_y(12, 0, 2, True)
+            make_y(14)
+            store_y(14)
+            round_y(13, 0, 1, False)
+            copy_y(11)
+            square_v(15, 0)
+            transpose_y(12)
+            multiply(15, 1)
+            quantize_y(10, 2)
+            store_codes(8, 12)
+            store_scales(0, 12, [nc.sync])
+            round_y(13, 1, 2, True)
+            round_y(14, 1, 2, True)
+            make_y(15, 0, 512)
+            store_y(15, 0, 512)
+            copy_y(12)
+            round_y(14, 0, 1, False)
+            square_v(15, 1)
+            transpose_y(13)
+            transpose_y(14)
+            make_y(15, 512, D)
+            store_y(15, 512, D)
+            copy_y(13)
+            round_y(15, 0, 1, False)
+            transpose_y(15, 0, 1)
+            copy_y(14)
+            quantize_y(12, 2, 0, 1)
+            round_y(15, 1, 2, True)
+            quantize_y(12, 2, 1, 2)
+            store_codes(12, 14)
+            transpose_y(15, 1, 2)
+            copy_y(15)
+            quantize_y(14, 1)
+            quantize_y(15, 1)
+            store_codes(14, 16)
+            store_scales(12, 16, [nc.scalar, nc.sync])

@@ -21,12 +21,12 @@ TILES = A // P
 KG = K // 512
 DG = D // 512
 NU = 12
-NW = 8
+NW = 6
 NS = 4
-NY = 8
+NY = 10
 NR = 4
-NA = 12
-CODE_GROUPS = ((0, 4), (4, 8), (8, 12), (12, 14), (14, 16))
+NA = 16
+CODE_GROUPS = ((0, 4), (4, 8), (8, 10), (10, 12), (12, 14), (14, 16))
 SCALE_GROUPS = ((0, 12), (12, 16))
 
 
@@ -39,7 +39,7 @@ def tile_dipole_gram_transfer_flow_k2_kernel(
         ps = ctx.enter_context(tc.psum_pool(name="ps", bufs=1))
 
         def sbuf(label, shape, dtype):
-            t = sb.tile(shape, dtype, name=label, align_bytes=64)
+            t = sb.tile(shape, dtype, name=label, align_bytes=256)
             return t
 
         def bank(label):
@@ -99,10 +99,11 @@ def tile_dipole_gram_transfer_flow_k2_kernel(
                         acc_bank[(n // 2) % 3][:, col : col + P], words[:, 256 * g + u : 256 * (g + 1) : 2], ident[:]
                     )
 
-        def copy_acc(n0, n1):
+        def copy_acc(n0, n1, on_vector=False):
             src = acc_bank[(n0 // 2) % 3][:].rearrange("p (n u m) -> p n m u", n=2, u=2)
             dst = acc_grp[:].bitcast(F32)
-            nc.scalar.copy(out=dst[:, n0 % NU : n0 % NU + n1 - n0, :, :], in_=src[:, n0 % 2 : n0 % 2 + n1 - n0, :, :])
+            move = nc.vector.tensor_copy if on_vector else nc.scalar.copy
+            move(out=dst[:, n0 % NU : n0 % NU + n1 - n0, :, :], in_=src[:, n0 % 2 : n0 % 2 + n1 - n0, :, :])
 
         def quantize_acc(n0, n1):
             span = slice(n0 % NU, n0 % NU + n1 - n0)
@@ -162,10 +163,11 @@ def tile_dipole_gram_transfer_flow_k2_kernel(
             for c in range(2 * g0, 2 * g1):
                 nc.tensor.transpose(y_bank[i % 2][:, P * c : P * (c + 1)], words[:, P * c : P * (c + 1)], ident[:])
 
-        def copy_y(i, g0=0, g1=DG):
+        def copy_y(i, g0=0, g1=DG, on_vector=False):
             dst = y_grp[(i // 2) % 2][:].bitcast(F32)[:, g0:g1, rows(i % 2), :]
             src = y_bank[i % 2][:].rearrange("p (g u m) -> p g m u", g=DG, u=2)[:, g0:g1, :, :]
-            nc.scalar.copy(out=dst, in_=src)
+            move = nc.vector.tensor_copy if on_vector else nc.scalar.copy
+            move(out=dst, in_=src)
 
         def quantize_y(i, n, g0=0, g1=DG):
             codes, code_lo = y_codes[i]
@@ -188,19 +190,43 @@ def tile_dipole_gram_transfer_flow_k2_kernel(
                     in_=y_sc[lo][0][32 * q : 32 * q + 4, :, :].bitcast(I32),
                 )
 
-        with tc.manual_schedule():
+        def clear_g_scales():
             nc.vector.memset(g_sc[:].bitcast(I32), 0)
-            make_identity(nc, ident[:])
+
+        def load_pop():
             nc.sync.dma_start(out=pop_rows[:], in_=donor_pop.rearrange("(p j) -> p j", j=8))
-            load_acc(0)
-            for q in range(4):
-                nc.scalar.dma_start(
-                    out=g_sc[32 * q : 32 * q + 4, :, :].bitcast(I32),
-                    in_=g_scales[:, 4 * q : 4 * q + 4, :].rearrange("g r n -> r g n").bitcast(I32),
+
+        def load_g_scales(q):
+            nc.sync.dma_start(
+                out=g_sc[32 * q : 32 * q + 4, :, :].bitcast(I32),
+                in_=g_scales[:, 4 * q : 4 * q + 4, :].rearrange("g r n -> r g n").bitcast(I32),
+            )
+
+        def spread_pop():
+            pop_words = pop_rows[:].bitcast(F32)
+            for j in range(4):
+                nc.tensor.transpose(
+                    y_bank[1][:, P * j : P * (j + 1)], pop_words[:, j : j + 1].to_broadcast([P, P]), ident[:]
                 )
+
+        def move_pop():
+            nc.scalar.copy(
+                out=pop_all[:, 0, :].bitcast(F32).rearrange("p (n j) -> p n j", j=4),
+                in_=y_bank[1][:].rearrange("p (j n) -> p n j", j=4),
+            )
+
+        with tc.manual_schedule():
+            make_identity(nc, ident[:])
+            clear_g_scales()
+            load_pop()
+            load_acc(0)
             load_inv(0)
             load_acc(1)
             load_acc(2)
+            load_g_scales(0)
+            load_g_scales(1)
+            load_g_scales(2)
+            load_g_scales(3)
             load_g(0)
             load_inv(1)
             load_inv(2)
@@ -223,21 +249,16 @@ def tile_dipole_gram_transfer_flow_k2_kernel(
             load_inv(10)
             load_acc(11)
             load_inv(11)
+            load_acc(12)
             load_inv(12)
+            load_acc(13)
             load_inv(13)
+            load_acc(14)
             load_inv(14)
+            load_acc(15)
             load_inv(15)
-
-            pop_words = pop_rows[:].bitcast(F32)
-            for j in range(4):
-                nc.tensor.transpose(
-                    y_bank[1][:, P * j : P * (j + 1)], pop_words[:, j : j + 1].to_broadcast([P, P]), ident[:]
-                )
-            nc.scalar.copy(
-                out=pop_all[:, 0, :].bitcast(F32).rearrange("p (n j) -> p n j", j=4),
-                in_=y_bank[1][:].rearrange("p (j n) -> p n j", j=4),
-            )
-
+            spread_pop()
+            move_pop()
             transpose_acc(0, 6)
             copy_acc(0, 2)
             copy_acc(2, 4)
@@ -326,74 +347,69 @@ def tile_dipole_gram_transfer_flow_k2_kernel(
                     store_codes(a - 6, a - 2)
                 make_y(b)
                 store_y(b)
-                if j < 4:
-                    load_acc(a + 8)
-                    load_acc(b + 8)
             transpose_acc(42, 48)
             transpose_y(8)
             transpose_y(9)
             copy_acc(42, 44)
             copy_acc(44, 46)
             copy_acc(46, 48)
-            round_y(10, 0, 1, True)
             quantize_acc(42, 44)
             round_y(11, 0, 2, True)
             quantize_acc(44, 48)
-            round_y(10, 1, 2, False)
+            copy_y(8)
             multiply(12, 0)
             square_v(12, 0)
             multiply(12, 1)
-            copy_y(8)
+            copy_y(9)
             square_v(12, 1)
             multiply(13, 0)
             multiply(13, 1)
+            round_y(10, 0, 1, False)
             square_v(13, 0)
             square_v(13, 1)
-            copy_y(9)
-            transpose_y(10)
-            make_y(12)
-            store_y(12)
-            make_y(13)
-            store_y(13)
-            quantize_y(8, 2)
+            round_y(10, 1, 2, False)
             multiply(14, 0)
             multiply(14, 1)
-            copy_y(10)
+            make_y(12)
+            store_y(12)
+            quantize_y(8, 2)
+            store_codes(8, 10)
+            make_y(13)
+            store_y(13)
             square_v(14, 0)
             square_v(14, 1)
             transpose_y(11)
+            transpose_y(10)
             multiply(15, 0)
+            multiply(15, 1)
             round_y(12, 0, 2, True)
             make_y(14)
             store_y(14)
-            round_y(13, 0, 1, False)
             copy_y(11)
+            copy_y(10)
             square_v(15, 0)
-            transpose_y(12)
-            multiply(15, 1)
+            round_y(13, 1, 2, False)
+            square_v(15, 1)
+            round_y(13, 0, 1, True)
             quantize_y(10, 2)
-            store_codes(8, 12)
+            store_codes(10, 12)
             store_scales(0, 12, [nc.sync])
-            round_y(13, 1, 2, True)
-            round_y(14, 1, 2, True)
+            transpose_y(12)
+            transpose_y(13)
+            round_y(14, 0, 2, True)
             make_y(15, 0, 512)
             store_y(15, 0, 512)
-            copy_y(12)
-            round_y(14, 0, 1, False)
-            square_v(15, 1)
-            transpose_y(13)
-            transpose_y(14)
             make_y(15, 512, D)
             store_y(15, 512, D)
+            copy_y(12)
             copy_y(13)
-            round_y(15, 0, 1, False)
-            transpose_y(15, 0, 1)
-            copy_y(14)
-            quantize_y(12, 2, 0, 1)
+            round_y(15, 0, 1, True)
             round_y(15, 1, 2, True)
-            quantize_y(12, 2, 1, 2)
+            transpose_y(14)
+            transpose_y(15)
+            quantize_y(12, 2)
             store_codes(12, 14)
-            transpose_y(15, 1, 2)
+            copy_y(14)
             copy_y(15)
             quantize_y(14, 1)
             quantize_y(15, 1)

from contextlib import ExitStack

import concourse.mybir as mybir
from concourse.masks import make_identity

A, D, K = 2048, 1024, 1536
FLOPS = 2 * A * D * K

F32 = mybir.dt.float32
BF16 = mybir.dt.bfloat16
I32 = mybir.dt.int32
U32 = mybir.dt.uint32
U8 = mybir.dt.uint8
E4M3X4 = mybir.dt.float8_e4m3fn_x4
E5M2X4 = mybir.dt.float8_e5m2_x4
SQUARE = mybir.ActivationFunctionType.Square
MULT = mybir.AluOpType.mult

P = 128
TILES = A // P
KG = K // 512
DG = D // 512
NU = 12
NW = 6
NS = 4
NY = 10
NR = 4
NA = 16
CODE_GROUPS = ((0, 4), (4, 8), (8, 10), (10, 12), (12, 14), (14, 16))
SCALE_GROUPS = ((0, 12), (12, 16))


def tile_dipole_gram_transfer_flow_k2_kernel(
    tc, g_words, g_scales, acceptor_dipoles, inv6, donor_pop, out_0, out_1, out_2
):
    nc = tc.nc
    with ExitStack() as ctx:
        sb = ctx.enter_context(tc.tile_pool(name="sb", bufs=1))
        ps = ctx.enter_context(tc.psum_pool(name="ps", bufs=1))

        def sbuf(label, shape, dtype):
            t = sb.tile(shape, dtype, name=label, align_bytes=256)
            return t

        def bank(label):
            t = ps.tile([P, 512], F32, name=label)
            return t

        ident = sbuf("ident", [P, P], F32)
        pop_rows = sbuf("pop_rows", [P, 8], BF16)
        pop_all = sbuf("pop_all", [P, 1, D], BF16)
        g_codes = [sbuf("g_codes%d" % h, [P, KG, 512], U32) for h in range(DG)]
        g_sc = sbuf("g_sc", [P, KG, D], U8)
        acc_raw = sbuf("acc_raw", [P, NA, K], BF16)
        inv_raw = sbuf("inv_raw", [P, TILES, D], BF16)
        acc_grp = sbuf("acc_grp", [P, NU, P, 4], BF16)
        acc_codes = sbuf("acc_codes", [P, NU, P], U32)
        acc_sc = sbuf("acc_sc", [P, NU, P], U8)
        weight = sbuf("weight", [P, NW, D], F32)
        square = sbuf("square", [P, NS, D], F32)
        y32 = sbuf("y32", [P, NY, D], F32)
        y16 = sbuf("y16", [P, NR, D], BF16)
        y_grp = [sbuf("y_grp%d" % j, [P, DG, 2 * P, 4], BF16) for j in range(2)]
        y_codes = {}
        for lo, hi in CODE_GROUPS:
            t = sbuf("y_codes%d" % lo, [P, DG, P * (hi - lo)], U32)
            for i in range(lo, hi):
                y_codes[i] = (t, lo)
        y_sc = {}
        for lo, hi in SCALE_GROUPS:
            t = sbuf("y_sc%d" % lo, [P, DG, P * (hi - lo)], U8)
            for i in range(lo, hi):
                y_sc[i] = (t, lo)

        acc_bank = [bank("acc_bank%d" % j) for j in range(3)]
        y_bank = [bank("y_bank%d" % j) for j in range(2)]
        v_bank = [bank("v_bank%d" % j) for j in range(3)]

        def rows(i, n=1):
            return slice(i * P, (i + n) * P)

        def load_acc(i):
            nc.sync.dma_start(out=acc_raw[:, i % NA, :], in_=acceptor_dipoles[rows(i), :])

        def load_inv(i):
            nc.sync.dma_start(out=inv_raw[:, i, :], in_=inv6[rows(i), :])

        def load_g(h):
            src = g_words.rearrange("g p n t -> p g (n t)")[:, :, 2048 * h : 2048 * (h + 1)]
            nc.sync.dma_start(out=g_codes[h][:].bitcast(I32), in_=src.bitcast(I32))

        def transpose_acc(n0, n1):
            for n in range(n0, n1):
                i, g = divmod(n, KG)
                words = acc_raw[:, i % NA, :].bitcast(F32)
                for u in range(2):
                    col = P * (2 * (n % 2) + u)
                    nc.tensor.transpose(
                        acc_bank[(n // 2) % 3][:, col : col + P], words[:, 256 * g + u : 256 * (g + 1) : 2], ident[:]
                    )

        def copy_acc(n0, n1, on_vector=False):
            src = acc_bank[(n0 // 2) % 3][:].rearrange("p (n u m) -> p n m u", n=2, u=2)
            dst = acc_grp[:].bitcast(F32)
            move = nc.vector.tensor_copy if on_vector else nc.scalar.copy
            move(out=dst[:, n0 % NU : n0 % NU + n1 - n0, :, :], in_=src[:, n0 % 2 : n0 % 2 + n1 - n0, :, :])

        def quantize_acc(n0, n1):
            span = slice(n0 % NU, n0 % NU + n1 - n0)
            nc.vector.quantize_mx(
                out=acc_codes[:, span, :].rearrange("p n m -> p (n m)").bitcast(E4M3X4),
                scales=acc_sc[:, span, :].rearrange("p n m -> p (n m)"),
                in_=acc_grp[:, span, :, :].rearrange("p n m t -> p (n m t)"),
            )

        def multiply(i, h):
            for g in range(KG):
                n = (KG * i + g) % NU
                nc.tensor.matmul_mx(
                    out=v_bank[(2 * i + h) % 3][:],
                    lhsT=acc_codes[:, n, :].bitcast(E4M3X4),
                    lhsT_scale=acc_sc[:, n, :],
                    rhs=g_codes[h][:, g, :].bitcast(E5M2X4),
                    rhs_scale=g_sc[:, g, 512 * h : 512 * (h + 1)],
                    start=(g == 0),
                    stop=(g == KG - 1),
                )

        def make_weight(i, n):
            nc.vector.tensor_tensor(
                out=weight[:, i % NW : i % NW + n, :],
                in0=inv_raw[:, i : i + n, :],
                in1=pop_all[:].to_broadcast([P, n, D]),
                op=MULT,
            )

        def square_v(i, h):
            nc.scalar.activation(
                out=square[:, i % NS, 512 * h : 512 * (h + 1)], in_=v_bank[(2 * i + h) % 3][:], func=SQUARE
            )

        def make_y(i, lo=0, hi=D):
            nc.vector.tensor_tensor(
                out=y32[:, i % NY, lo:hi], in0=square[:, i % NS, lo:hi], in1=weight[:, i % NW, lo:hi], op=MULT
            )

        def store_y(i, lo=0, hi=D):
            nc.sync.dma_start(out=out_0[rows(i), lo:hi], in_=y32[:, i % NY, lo:hi])

        def round_y(i, g0, g1, on_vector):
            src = y32[:, i % NY, 512 * g0 : 512 * g1].rearrange("a (g p u e) -> a g u p e", p=P, u=2, e=2)
            dst = y16[:, i % NR, 512 * g0 : 512 * g1].rearrange("a (g u p e) -> a g u p e", p=P, u=2, e=2)
            if g1 - g0 == 1:
                src = src[:, 0, :, :, :]
                dst = dst[:, 0, :, :, :]
            if on_vector:
                nc.vector.tensor_copy(out=dst, in_=src)
            else:
                nc.scalar.copy(out=dst, in_=src)

        def transpose_y(i, g0=0, g1=DG):
            words = y16[:, i % NR, :].bitcast(F32)
            for c in range(2 * g0, 2 * g1):
                nc.tensor.transpose(y_bank[i % 2][:, P * c : P * (c + 1)], words[:, P * c : P * (c + 1)], ident[:])

        def copy_y(i, g0=0, g1=DG, on_vector=False):
            dst = y_grp[(i // 2) % 2][:].bitcast(F32)[:, g0:g1, rows(i % 2), :]
            src = y_bank[i % 2][:].rearrange("p (g u m) -> p g m u", g=DG, u=2)[:, g0:g1, :, :]
            move = nc.vector.tensor_copy if on_vector else nc.scalar.copy
            move(out=dst, in_=src)

        def quantize_y(i, n, g0=0, g1=DG):
            codes, code_lo = y_codes[i]
            scales, scale_lo = y_sc[i]
            for g in range(g0, g1):
                nc.vector.quantize_mx(
                    out=codes[:, g, rows(i - code_lo, n)].bitcast(E4M3X4),
                    scales=scales[:, g, rows(i - scale_lo, n)],
                    in_=y_grp[(i // 2) % 2][:, g, rows(i % 2, n), :].rearrange("p m t -> p (m t)"),
                )

        def store_codes(lo, hi):
            dst = out_1.rearrange("g p m t -> p g (m t)")[:, :, 4 * P * lo : 4 * P * hi]
            nc.sync.dma_start(out=dst.bitcast(I32), in_=y_codes[lo][0][:].bitcast(I32))

        def store_scales(lo, hi, engines):
            for q in range(4):
                engines[q % len(engines)].dma_start(
                    out=out_2[:, 4 * q : 4 * q + 4, P * lo : P * hi].rearrange("g r m -> r g m").bitcast(I32),
                    in_=y_sc[lo][0][32 * q : 32 * q + 4, :, :].bitcast(I32),
                )

        def clear_g_scales():
            nc.vector.memset(g_sc[:].bitcast(I32), 0)

        def load_pop():
            nc.sync.dma_start(out=pop_rows[:], in_=donor_pop.rearrange("(p j) -> p j", j=8))

        def load_g_scales(q):
            nc.sync.dma_start(
                out=g_sc[32 * q : 32 * q + 4, :, :].bitcast(I32),
                in_=g_scales[:, 4 * q : 4 * q + 4, :].rearrange("g r n -> r g n").bitcast(I32),
            )

        def spread_pop():
            pop_words = pop_rows[:].bitcast(F32)
            for j in range(4):
                nc.tensor.transpose(
                    y_bank[1][:, P * j : P * (j + 1)], pop_words[:, j : j + 1].to_broadcast([P, P]), ident[:]
                )

        def move_pop():
            nc.scalar.copy(
                out=pop_all[:, 0, :].bitcast(F32).rearrange("p (n j) -> p n j", j=4),
                in_=y_bank[1][:].rearrange("p (j n) -> p n j", j=4),
            )

        with tc.manual_schedule():
            make_identity(nc, ident[:])
            clear_g_scales()
            load_pop()
            load_acc(0)
            load_inv(0)
            load_acc(1)
            load_acc(2)
            load_g_scales(0)
            load_g_scales(1)
            load_g_scales(2)
            load_g_scales(3)
            load_g(0)
            load_inv(1)
            load_inv(2)
            load_inv(3)
            load_acc(3)
            load_g(1)
            load_inv(4)
            load_acc(4)
            load_acc(5)
            load_inv(5)
            load_inv(6)
            load_inv(7)
            load_acc(6)
            load_acc(7)
            load_acc(8)
            load_inv(8)
            load_acc(9)
            load_inv(9)
            load_acc(10)
            load_inv(10)
            load_acc(11)
            load_inv(11)
            load_acc(12)
            load_inv(12)
            load_acc(13)
            load_inv(13)
            load_acc(14)
            load_inv(14)
            load_acc(15)
            load_inv(15)
            spread_pop()
            move_pop()
            transpose_acc(0, 6)
            copy_acc(0, 2)
            copy_acc(2, 4)
            copy_acc(4, 6)
            make_weight(0, 1)
            quantize_acc(0, 2)
            quantize_acc(2, 4)
            transpose_acc(6, 8)
            copy_acc(6, 8)
            quantize_acc(4, 6)
            make_weight(1, 1)
            multiply(0, 0)
            multiply(1, 0)
            transpose_acc(8, 12)
            square_v(0, 0)
            square_v(1, 0)
            make_weight(2, 1)
            make_weight(3, 1)
            copy_acc(8, 10)
            copy_acc(10, 12)
            make_y(0, 0, 512)
            make_y(1, 0, 512)
            quantize_acc(6, 8)
            quantize_acc(8, 12)
            multiply(0, 1)
            multiply(1, 1)
            transpose_acc(12, 18)
            round_y(0, 0, 1, False)
            square_v(0, 1)
            round_y(1, 0, 1, False)
            square_v(1, 1)
            make_weight(4, 1)
            make_y(0, 512, D)
            make_y(1, 512, D)
            store_y(0)
            store_y(1)
            copy_acc(12, 14)
            copy_acc(14, 16)
            round_y(0, 1, 2, False)
            copy_acc(16, 18)
            multiply(2, 0)
            square_v(2, 0)
            multiply(2, 1)
            round_y(1, 1, 2, False)
            square_v(2, 1)
            multiply(3, 0)
            multiply(3, 1)
            square_v(3, 0)
            square_v(3, 1)
            make_weight(5, 1)
            quantize_acc(12, 14)
            make_weight(6, 2)
            quantize_acc(14, 18)
            make_y(2)
            make_y(3)
            store_y(2)
            store_y(3)
            for j in range(2, 6):
                a, b, n = 2 * j, 2 * j + 1, 6 * j
                transpose_acc(n + 6, n + 12)
                transpose_y(a - 4)
                transpose_y(b - 4)
                copy_acc(n + 6, n + 8)
                copy_acc(n + 8, n + 10)
                copy_acc(n + 10, n + 12)
                round_y(a - 2, 0, 1, False)
                round_y(a - 2, 1, 2, False)
                quantize_acc(n + 6, n + 8)
                round_y(b - 2, 0, 2, True)
                make_weight(a + 4, 2)
                quantize_acc(n + 8, n + 12)
                multiply(a, 0)
                square_v(a, 0)
                multiply(a, 1)
                copy_y(b - 4)
                square_v(a, 1)
                copy_y(a - 4)
                multiply(b, 0)
                multiply(b, 1)
                square_v(b, 0)
                square_v(b, 1)
                make_y(a)
                store_y(a)
                quantize_y(a - 4, 2)
                if j % 2 == 1:
                    store_codes(a - 6, a - 2)
                make_y(b)
                store_y(b)
            transpose_acc(42, 48)
            transpose_y(8)
            transpose_y(9)
            copy_acc(42, 44)
            copy_acc(44, 46)
            copy_acc(46, 48)
            quantize_acc(42, 44)
            round_y(11, 0, 2, True)
            quantize_acc(44, 48)
            copy_y(8)
            multiply(12, 0)
            square_v(12, 0)
            multiply(12, 1)
            copy_y(9)
            square_v(12, 1)
            multiply(13, 0)
            multiply(13, 1)
            round_y(10, 0, 1, False)
            square_v(13, 0)
            square_v(13, 1)
            round_y(10, 1, 2, False)
            multiply(14, 0)
            multiply(14, 1)
            make_y(12)
            store_y(12)
            quantize_y(8, 2)
            store_codes(8, 10)
            make_y(13)
            store_y(13)
            square_v(14, 0)
            square_v(14, 1)
            transpose_y(11)
            transpose_y(10)
            multiply(15, 0)
            multiply(15, 1)
            round_y(12, 0, 2, True)
            make_y(14)
            store_y(14)
            copy_y(11)
            copy_y(10)
            square_v(15, 0)
            round_y(13, 1, 2, False)
            square_v(15, 1)
            round_y(13, 0, 1, True)
            quantize_y(10, 2)
            store_codes(10, 12)
            store_scales(0, 12, [nc.sync])
            transpose_y(12)
            transpose_y(13)
            round_y(14, 0, 2, True)
            make_y(15, 0, 512)
            store_y(15, 0, 512)
            make_y(15, 512, D)
            store_y(15, 512, D)
            copy_y(12)
            copy_y(13)
            round_y(15, 0, 1, True)
            round_y(15, 1, 2, True)
            transpose_y(14)
            transpose_y(15)
            quantize_y(12, 2)
            store_codes(12, 14)
            copy_y(14)
            copy_y(15)
            quantize_y(14, 1)
            quantize_y(15, 1)
            store_codes(14, 16)
            store_scales(12, 16, [nc.scalar, nc.sync])
